import numpy as np
import ml_dtypes


def mxq(x, axis, fmt="e4m3"):
    dtype, down = {"e4m3": (ml_dtypes.float8_e4m3fn, 7), "e5m2": (ml_dtypes.float8_e5m2, 14)}[fmt]
    v = np.moveaxis(np.asarray(x, np.float32).astype(ml_dtypes.bfloat16).astype(np.float64), axis, -1)
    blocks = v.reshape(v.shape[:-1] + (-1, 32))
    amax = np.abs(blocks).max(-1, keepdims=True)
    byte = np.maximum(np.where(amax > 0, np.frexp(amax)[1] - 1 + 127, 0) - down, 1)
    scale = np.exp2(byte - 127.0)
    codes = (blocks / scale).astype(np.float32).astype(dtype).astype(np.float64)
    return np.moveaxis((codes * scale).reshape(v.shape), -1, axis)


WIDE = False


def mx_kscale(k):
    if not WIDE:
        return np.ones(k)
    levels = np.array([30, -30])
    if k % 512:
        return np.exp2(np.random.permutation(np.resize(levels, k // 32))).repeat(32)
    a = np.empty((k // 512, 16))
    for p in range(k // 512):
        a[p, :8] = np.random.permutation(np.resize(levels, 8))
        for g in range(8):
            far = levels[np.abs(levels - a[p, g]) >= 10]
            a[p, g + 8] = far[np.random.randint(len(far))]
    return np.exp2(a.ravel()).repeat(32)


def f64(x):
    return np.asarray(x).astype(np.float64)


def striped(idx):
    return np.tile(np.asarray(idx).reshape(-1, 16).T, (8, 1)).astype(np.uint16)


def unstriped(offs):
    return offs[:16].T.reshape(-1).astype(np.int64)


def striped8(idx):
    return np.asarray(idx).reshape(8, -1, 16).transpose(0, 2, 1).reshape(128, -1).astype(np.uint16)


def unstriped8(offs):
    return offs.reshape(8, 16, -1).transpose(0, 2, 1).reshape(8, -1).astype(np.int64)


def pick8(x, idx, run):
    r = np.arange(len(x))
    return x[r[:, None], idx[r % (8 * run) // run]]


E2M1 = np.array([0.0, 0.5, 1.0, 1.5, 2.0, 3.0, 4.0, 6.0, -0.0, -0.5, -1.0, -1.5, -2.0, -3.0, -4.0, -6.0])


def pack_weight(w, fmt):
    k, n = w.shape
    w = f64(np.asarray(w, np.float32).astype(ml_dtypes.bfloat16)).reshape(k // 32, 32, n)
    amax = np.abs(w).max(1)
    if fmt in ("e4m3", "e5m2"):
        byte = np.frexp(amax)[1] - 1 + 127 - (7 if fmt == "e4m3" else 14)
    else:
        mant, ex = np.frexp(amax / 6.0)
        byte = np.where(mant > 0.5, ex, ex - 1) + 127
    byte = np.clip(np.where(amax > 0, byte, 1), 1, 254)
    scaled = (w * np.exp2(127.0 - byte)[:, None, :]).reshape(k, n).astype(np.float32)
    by_word = np.ascontiguousarray(scaled.reshape(k // 512, 128, 4, n).transpose(0, 1, 3, 2))
    if fmt in ("e4m3", "e5m2"):
        words = by_word.astype(ml_dtypes.float8_e4m3fn if fmt == "e4m3" else ml_dtypes.float8_e5m2).view(np.uint8)
    else:
        c = by_word.astype(ml_dtypes.float4_e2m1fn).view(np.uint8) & 0xF
        words = (c[..., 0::2] | (c[..., 1::2] << 4)).reshape(k // 512, 128, 2 * n)
    return np.ascontiguousarray(words), np.ascontiguousarray(byte.astype(np.uint8).reshape(k // 512, 16, n))


def unpack_weight(words, scales, fmt):
    g, _, n = scales.shape
    words = np.ascontiguousarray(words).reshape(g, 128, n, -1)
    if fmt in ("e4m3", "e5m2"):
        vals = words.view(ml_dtypes.float8_e4m3fn if fmt == "e4m3" else ml_dtypes.float8_e5m2).astype(np.float64)
    else:
        nib = np.empty((g, 128, n, 4), np.uint8)
        nib[..., 0::2] = words & 0xF
        nib[..., 1::2] = words >> 4
        vals = E2M1[nib]
    vals = vals * np.repeat(np.exp2(scales.astype(np.float64) - 127.0), 8, axis=1)[..., None]
    return vals.transpose(0, 1, 3, 2).reshape(g * 512, n)


K, T, J, R, F, Z, C, I, O, N = 512, 1024, 256, 512, 512, 1024, 512, 128, 128, 256


def setup_inputs():
    n = np.random.standard_normal
    idx = np.random.permutation(T)[:J]
    idx2 = np.random.permutation(Z)[:J]
    idx3 = np.random.permutation(J)[:I]
    idx4 = np.stack([np.random.permutation(C)[:I] for _ in range(8)])
    idx5 = np.random.permutation(C)[:O]
    idx6 = np.random.permutation(J)[:O]
    idx7 = np.random.permutation(T)[:O]
    fk = mx_kscale(K)
    ff = mx_kscale(F)
    fr = mx_kscale(R)
    xtp = pack_weight(n((K, T)) / fk[:, None], "e5m2")
    xop = pack_weight(n((F, Z)) / ff[:, None], "e4m3")
    wp = pack_weight(n((K, R)) * 1 / np.sqrt(K) * fk[:, None] * fr, "e2m1")
    w2p = pack_weight(n((K, R)) * 1 / np.sqrt(K) * fk[:, None] * fr, "e4m3")
    w0p = pack_weight(n((F, R)) * 1 / np.sqrt(F) * ff[:, None] * fr, "e4m3")
    wbp = pack_weight(n((R, N)) * 1 / np.sqrt(R) / fr[:, None], "e2m1")
    wsp = pack_weight(n((K, N)) * 1 / np.sqrt(K) * fk[:, None], "e2m1")
    return {
        "xt_words": xtp[0],
        "xt_scales": xtp[1],
        "xo_words": xop[0],
        "xo_scales": xop[1],
        "w_words": wp[0],
        "w_scales": wp[1],
        "w2_words": w2p[0],
        "w2_scales": w2p[1],
        "w0_words": w0p[0],
        "w0_scales": w0p[1],
        "sa": (np.random.uniform(0.5, 1.6, (R, 1))).astype(np.float32),
        "sb": (np.random.uniform(0.5, 1.6, (R, 1))).astype(np.float32),
        "wb_words": wbp[0],
        "wb_scales": wbp[1],
        "ws_words": wsp[0],
        "ws_scales": wsp[1],
        "offs": striped(idx),
        "offs2": striped(idx2),
        "offs3": striped(idx3),
        "offs4": striped8(idx4),
        "offs5": striped(idx5),
        "offs6": striped(idx6),
        "offs7": striped(idx7),
    }


def reference(xt_words, xt_scales, xo_words, xo_scales, w_words, w_scales, w2_words, w2_scales, w0_words, w0_scales, sa, sb, wb_words, wb_scales, ws_words, ws_scales, offs, offs2, offs3, offs4, offs5, offs6, offs7):
    idx = unstriped(offs)
    idx2 = unstriped(offs2)
    idx3 = unstriped(offs3)
    idx4 = unstriped8(offs4)
    idx5 = unstriped(offs5)
    idx6 = unstriped(offs6)
    idx7 = unstriped(offs7)
    xtu = unpack_weight(xt_words, xt_scales, "e5m2")
    xou = unpack_weight(xo_words, xo_scales, "e4m3")
    wu = unpack_weight(w_words, w_scales, "e2m1")
    w2u = unpack_weight(w2_words, w2_scales, "e4m3")
    w0u = unpack_weight(w0_words, w0_scales, "e4m3")
    wbu = unpack_weight(wb_words, wb_scales, "e2m1")
    wsu = unpack_weight(ws_words, ws_scales, "e2m1")
    xtidxg = xtu[:, idx]
    a = wu.T @ xtidxg
    xoidx2g = xou[:, idx2]
    b = w2u.T @ xtidxg + w0u.T @ xoidx2g
    h1 = a[:, idx3] * f64(sa)
    pw = np.zeros((R, C))
    pw[np.arange(R)[:, None], idx4[np.arange(R) % 512 // 64]] = h1
    hid = np.abs(pw[:, idx5] - b[:, idx6] * f64(sb))
    hidq = mxq(hid, 0, "e4m3")
    xtidx7g = xtu[:, idx7]
    y = wbu.T @ hidq + wsu.T @ xtidx7g
    return y

@@ -1,0 +1,185 @@
+from contextlib import ExitStack
+
+import concourse.mybir as mybir
+
+F32 = mybir.dt.float32
+BF16 = mybir.dt.bfloat16
+I32 = mybir.dt.int32
+U32 = mybir.dt.uint32
+U16 = mybir.dt.uint16
+U8 = mybir.dt.uint8
+E4M3 = mybir.dt.float8_e4m3fn_x4
+E5M2 = mybir.dt.float8_e5m2_x4
+E2M1 = mybir.dt.float4_e2m1fn_x4
+ALU = mybir.AluOpType
+ACT = mybir.ActivationFunctionType
+
+K, T, J, R, F, Z, C, I, O, N = 512, 1024, 256, 512, 512, 1024, 512, 128, 128, 256
+P = 128
+PACK = 4
+FLOPS = 2 * (3 * K * R * J + R * N * O + K * N * O)
+
+
+def tile_list_ownseats_leaned_further_plain_kernel(
+    tc, xt_words, xt_scales, xo_words, xo_scales, w_words, w_scales, w2_words, w2_scales, w0_words, w0_scales,
+    sa, sb, wb_words, wb_scales, ws_words, ws_scales, offs, offs2, offs3, offs4, offs5, offs6, offs7, out,
+):
+    nc = tc.nc
+    with ExitStack() as ctx:
+        keep = ctx.enter_context(tc.tile_pool(name="keep", bufs=1))
+        psum = ctx.enter_context(tc.psum_pool(name="psum", bufs=1))
+
+        def sbuf(name, shape, dtype):
+            return keep.tile(shape, dtype, name=name, align_bytes=64)
+
+        def load_list(name, src):
+            t = keep.tile(list(src.shape), U16, name=name)
+            nc.sync.dma_start(t[:], src)
+            return t
+
+        def fp8_rows(src):
+            return src[0].rearrange("p c r -> p (c r)").bitcast(I32)
+
+        def load_plane(plane, src, *engs):
+            rows = src[0].bitcast(I32)
+            for q in range(4):
+                engs[q % len(engs)].dma_start(plane[32 * q : 32 * q + 4].bitcast(I32), rows[4 * q : 4 * q + 4, :])
+
+        def stage_rows(dst, src, eng):
+            eng.dma_start(dst, src[0].bitcast(I32).rearrange("(q r) w -> r q w", r=4))
+
+        def spread(plane, staged):
+            for q in range(4):
+                nc.vector.tensor_copy(plane[32 * q : 32 * q + 4, :].bitcast(I32), staged[:, q, :])
+
+        xt_s = sbuf("xt_s", [P, T], U8)
+        xo_s = sbuf("xo_s", [P, Z], U8)
+        w_sr = sbuf("w_sr", [P, R], U8)
+        w20_sr = sbuf("w20_sr", [P, 2 * R], U8)
+        wbs_s = sbuf("wbs_s", [P, 2 * N], U8)
+        pw = [sbuf("pw%d" % t, [P, C], F32) for t in range(PACK)]
+        for plane in (w_sr, xt_s, xo_s, w20_sr, wbs_s):
+            nc.vector.memset(plane[:].bitcast(I32), 0)
+        for t in range(PACK):
+            nc.gpsimd.memset(pw[t][:], 0.0)
+
+        xt_w = sbuf("xt_w", [P, T], U32)
+        xo_w = sbuf("xo_w", [P, Z], U32)
+        w_raw = sbuf("w_raw", [P, R], U16)
+        w2_raw = sbuf("w2_raw", [P, R], U32)
+        w0_raw = sbuf("w0_raw", [P, R], U32)
+        wb_w = sbuf("wb_w", [P, N], U16)
+        ws_w = sbuf("ws_w", [P, N], U16)
+        w_st = sbuf("w_st", [4, 4, R // 4], I32)
+        w20_st = sbuf("w20_st", [4, 4, 2 * R // 4], I32)
+        sa_t = sbuf("sa_t", [P, PACK], F32)
+        sb_t = sbuf("sb_t", [P, PACK], F32)
+
+        xt_st = sbuf("xt_st", [4, 4, T // 4], I32)
+        stage_rows(w_st[:], w_scales, nc.scalar)
+        stage_rows(xt_st[:], xt_scales, nc.sync)
+        l1 = load_list("l1", offs)
+        nc.scalar.dma_start(w_raw[:].bitcast(I32), w_words[0].bitcast(I32))
+        nc.sync.dma_start(xt_w[:].bitcast(I32), fp8_rows(xt_words))
+        nc.scalar.dma_start(sa_t[:], sa.rearrange("(p t) o -> p (t o)", t=PACK))
+        l3 = load_list("l3", offs3)
+        l4 = load_list("l4", offs4)
+        stage_rows(w20_st[:, :, 0 : R // 4], w2_scales, nc.sync)
+        stage_rows(w20_st[:, :, R // 4 :], w0_scales, nc.sync)
+        nc.sync.dma_start(w2_raw[:].bitcast(I32), fp8_rows(w2_words))
+        nc.sync.dma_start(w0_raw[:].bitcast(I32), fp8_rows(w0_words))
+        nc.sync.dma_start(xo_w[:].bitcast(I32), fp8_rows(xo_words))
+        l2 = load_list("l2", offs2)
+        load_plane(xo_s[:], xo_scales, nc.sync)
+        l7 = load_list("l7", offs7)
+        l6 = load_list("l6", offs6)
+        nc.sync.dma_start(sb_t[:], sb.rearrange("(p t) o -> p (t o)", t=PACK))
+        l5 = load_list("l5", offs5)
+        nc.sync.dma_start(ws_w[:].bitcast(I32), ws_words[0].bitcast(I32))
+        nc.sync.dma_start(wb_w[:].bitcast(I32), wb_words[0].bitcast(I32))
+        load_plane(wbs_s[:, N:], ws_scales, nc.sync)
+        load_plane(wbs_s[:, 0:N], wb_scales, nc.sync)
+
+        def deal(copy, dst, src, line):
+            copy(dst.rearrange("p (t c i) -> p c t i", t=PACK, i=line), src.rearrange("p (c i t) -> p c t i", t=PACK, i=line))
+
+        xg_s = sbuf("xg_s", [P, J], U8)
+        xg_w = sbuf("xg_w", [P, J], U32)
+        w_s = sbuf("w_s", [P, R], U8)
+        w_w = sbuf("w_w", [P, R], U16)
+        deal(nc.scalar.copy, w_w[:], w_raw[:], 8)
+        spread(w_sr, w_st)
+        deal(nc.gpsimd.tensor_copy, w_s[:], w_sr[:], 16)
+        spread(xt_s, xt_st)
+        nc.vector.tensor_copy(xg_s[:], xt_s[:].indirect(l1[:]))
+        nc.vector.tensor_copy(xg_w[:], xt_w[:].indirect(l1[:]))
+
+        a_sb = [sbuf("a%d" % t, [P, J], F32) for t in range(PACK)]
+        h1 = [sbuf("h%d" % t, [P, I], F32) for t in range(PACK)]
+        for t in range(PACK):
+            cols = slice(P * t, P * (t + 1))
+            acc = psum.tile([P, J], F32, name="acc", tag="acc", bufs=6)
+            nc.tensor.matmul_mx(acc[:], lhsT=w_w[:, cols].bitcast(E2M1), lhsT_scale=w_s[:, cols],
+                                rhs=xg_w[:].bitcast(E5M2), rhs_scale=xg_s[:], start=True, stop=True)
+            nc.vector.tensor_copy(a_sb[t][:], acc[:])
+        for t in range(PACK + 1):
+            if t < PACK:
+                nc.scalar.activation(h1[t][:], a_sb[t][:].indirect(l3[:]), ACT.Copy, scale=sa_t[:, t : t + 1])
+            if t > 0:
+                nc.scalar.activation(pw[t - 1][:].indirect(l4[:]), h1[t - 1][:], ACT.Copy)
+
+        w2_w = sbuf("w2_w", [P, R], U32)
+        w0_w = sbuf("w0_w", [P, R], U32)
+        w20_s = sbuf("w20_s", [P, 2 * R], U8)
+        og_s = sbuf("og_s", [P, J], U8)
+        og_w = sbuf("og_w", [P, J], U32)
+        spread(w20_sr, w20_st)
+        deal(nc.gpsimd.tensor_copy, w2_w[:], w2_raw[:], 4)
+        deal(nc.gpsimd.tensor_copy, w0_w[:], w0_raw[:], 4)
+        deal(nc.gpsimd.tensor_copy, w20_s[:, 0:R], w20_sr[:, 0:R], 16)
+        deal(nc.gpsimd.tensor_copy, w20_s[:, R:], w20_sr[:, R:], 16)
+        nc.vector.tensor_copy(og_w[:], xo_w[:].indirect(l2[:]))
+        nc.vector.tensor_copy(og_s[:], xo_s[:].indirect(l2[:]))
+        b_sb = [sbuf("b%d" % t, [P, J], F32) for t in range(PACK)]
+        for t in range(PACK):
+            cols = slice(P * t, P * (t + 1))
+            cols0 = slice(R + P * t, R + P * (t + 1))
+            acc = psum.tile([P, J], F32, name="acc", tag="acc", bufs=6)
+            nc.tensor.matmul_mx(acc[:], lhsT=w2_w[:, cols].bitcast(E4M3), lhsT_scale=w20_s[:, cols],
+                                rhs=xg_w[:].bitcast(E5M2), rhs_scale=xg_s[:], start=True, stop=False)
+            nc.tensor.matmul_mx(acc[:], lhsT=w0_w[:, cols].bitcast(E4M3), lhsT_scale=w20_s[:, cols0],
+                                rhs=og_w[:].bitcast(E4M3), rhs_scale=og_s[:], start=False, stop=True)
+            nc.vector.tensor_copy(b_sb[t][:], acc[:])
+
+        sg_s = sbuf("sg_s", [P, O], U8)
+        sg_w = sbuf("sg_w", [P, O], U32)
+        nc.vector.tensor_copy(sg_w[:], xt_w[:].indirect(l7[:]))
+        nc.vector.tensor_copy(sg_s[:], xt_s[:].indirect(l7[:]))
+        y = [psum.tile([P, O], F32, name="y%d" % h) for h in range(N // P)]
+        for h in range(N // P):
+            nc.tensor.matmul_mx(y[h][:], lhsT=ws_w[:, P * h : P * (h + 1)].bitcast(E2M1),
+                                lhsT_scale=wbs_s[:, N + P * h : N + P * (h + 1)],
+                                rhs=sg_w[:].bitcast(E5M2), rhs_scale=sg_s[:], start=True, stop=False)
+
+        bs = [sbuf("bs%d" % t, [P, O], F32) for t in range(PACK)]
+        diff = sbuf("diff", [P, PACK, O], F32)
+        for t in range(PACK):
+            nc.scalar.activation(bs[t][:], b_sb[t][:].indirect(l6[:]), ACT.Copy, scale=sb_t[:, t : t + 1])
+            nc.vector.tensor_tensor(diff[:, t, :], pw[t][:].indirect(l5[:]), bs[t][:], ALU.subtract)
+        hid = sbuf("hid", [P, O, PACK], BF16)
+        woven = diff[:].rearrange("p t o -> p o t")
+        half = O // 2
+        nc.scalar.activation(hid[:, 0:half, :], woven[:, 0:half, :], ACT.Abs)
+        nc.vector.scalar_tensor_tensor(hid[:, half:, :], woven[:, half:, :], -1.0, woven[:, half:, :], ALU.mult, ALU.max)
+        hq_w = sbuf("hq_w", [P, O], U32)
+        hq_s = sbuf("hq_s", [P, O], U8)
+        nc.vector.quantize_mx(hq_w[:].bitcast(E4M3), hq_s[:], hid[:].rearrange("p o t -> p (o t)"))
+        y_sb = [sbuf("ysb%d" % h, [P, O], F32) for h in range(N // P)]
+        for h in range(N // P):
+            nc.tensor.matmul_mx(y[h][:], lhsT=wb_w[:, P * h : P * (h + 1)].bitcast(E2M1),
+                                lhsT_scale=wbs_s[:, P * h : P * (h + 1)],
+                                rhs=hq_w[:].bitcast(E4M3), rhs_scale=hq_s[:], start=False, stop=True)
+        nc.vector.tensor_copy(y_sb[0][:], y[0][:])
+        nc.sync.dma_start(out[0:P, :], y_sb[0][:])
+        nc.scalar.copy(y_sb[1][:], y[1][:])
+        nc.scalar.dma_start(out[P:, :], y_sb[1][:])

@@ -55,13 +55,14 @@ def tile_list_ownseats_leaned_further_plain_kernel(
         xt_s = sbuf("xt_s", [P, T], U8)
         xo_s = sbuf("xo_s", [P, Z], U8)
         w_sr = sbuf("w_sr", [P, R], U8)
-        w20_sr = sbuf("w20_sr", [P, 2 * R], U8)
+        w2_sr = sbuf("w2_sr", [P, R], U8)
+        w0_sr = sbuf("w0_sr", [P, R], U8)
         wbs_s = sbuf("wbs_s", [P, 2 * N], U8)
         pw = [sbuf("pw%d" % t, [P, C], F32) for t in range(PACK)]
-        for plane in (w_sr, xt_s, xo_s, w20_sr, wbs_s):
+        for plane in (xt_s, w_sr, xo_s, w2_sr, w0_sr, wbs_s):
             nc.vector.memset(plane[:].bitcast(I32), 0)
         for t in range(PACK):
-            nc.gpsimd.memset(pw[t][:], 0.0)
+            nc.vector.memset(pw[t][:], 0.0)
 
         xt_w = sbuf("xt_w", [P, T], U32)
         xo_w = sbuf("xo_w", [P, Z], U32)
@@ -71,30 +72,28 @@ def tile_list_ownseats_leaned_further_plain_kernel(
         wb_w = sbuf("wb_w", [P, N], U16)
         ws_w = sbuf("ws_w", [P, N], U16)
         w_st = sbuf("w_st", [4, 4, R // 4], I32)
-        w20_st = sbuf("w20_st", [4, 4, 2 * R // 4], I32)
         sa_t = sbuf("sa_t", [P, PACK], F32)
         sb_t = sbuf("sb_t", [P, PACK], F32)
 
-        xt_st = sbuf("xt_st", [4, 4, T // 4], I32)
-        stage_rows(w_st[:], w_scales, nc.scalar)
-        stage_rows(xt_st[:], xt_scales, nc.sync)
         l1 = load_list("l1", offs)
-        nc.scalar.dma_start(w_raw[:].bitcast(I32), w_words[0].bitcast(I32))
-        nc.sync.dma_start(xt_w[:].bitcast(I32), fp8_rows(xt_words))
+        stage_rows(w_st[:], w_scales, nc.scalar)
+        nc.sync.dma_start(w_raw[:].bitcast(I32), w_words[0].bitcast(I32))
         nc.scalar.dma_start(sa_t[:], sa.rearrange("(p t) o -> p (t o)", t=PACK))
+        nc.scalar.dma_start(xt_w[:].bitcast(I32), fp8_rows(xt_words))
+        load_plane(xt_s[:], xt_scales, nc.sync)
         l3 = load_list("l3", offs3)
         l4 = load_list("l4", offs4)
-        stage_rows(w20_st[:, :, 0 : R // 4], w2_scales, nc.sync)
-        stage_rows(w20_st[:, :, R // 4 :], w0_scales, nc.sync)
+        l2 = load_list("l2", offs2)
+        l7 = load_list("l7", offs7)
         nc.sync.dma_start(w2_raw[:].bitcast(I32), fp8_rows(w2_words))
         nc.sync.dma_start(w0_raw[:].bitcast(I32), fp8_rows(w0_words))
         nc.sync.dma_start(xo_w[:].bitcast(I32), fp8_rows(xo_words))
-        l2 = load_list("l2", offs2)
+        load_plane(w2_sr[:], w2_scales, nc.sync)
+        load_plane(w0_sr[:], w0_scales, nc.sync)
         load_plane(xo_s[:], xo_scales, nc.sync)
-        l7 = load_list("l7", offs7)
         l6 = load_list("l6", offs6)
-        nc.sync.dma_start(sb_t[:], sb.rearrange("(p t) o -> p (t o)", t=PACK))
         l5 = load_list("l5", offs5)
+        nc.gpsimd.dma_start(sb_t[:], sb.rearrange("(p t) o -> p (t o)", t=PACK))
         nc.sync.dma_start(ws_w[:].bitcast(I32), ws_words[0].bitcast(I32))
         nc.sync.dma_start(wb_w[:].bitcast(I32), wb_words[0].bitcast(I32))
         load_plane(wbs_s[:, N:], ws_scales, nc.sync)
@@ -109,10 +108,13 @@ def tile_list_ownseats_leaned_further_plain_kernel(
         w_w = sbuf("w_w", [P, R], U16)
         deal(nc.scalar.copy, w_w[:], w_raw[:], 8)
         spread(w_sr, w_st)
-        deal(nc.gpsimd.tensor_copy, w_s[:], w_sr[:], 16)
-        spread(xt_s, xt_st)
+        deal(nc.vector.tensor_copy, w_s[:], w_sr[:], 16)
         nc.vector.tensor_copy(xg_s[:], xt_s[:].indirect(l1[:]))
         nc.vector.tensor_copy(xg_w[:], xt_w[:].indirect(l1[:]))
+        w2_w = sbuf("w2_w", [P, R], U32)
+        w0_w = sbuf("w0_w", [P, R], U32)
+        deal(nc.scalar.copy, w2_w[:], w2_raw[:], 4)
+        deal(nc.scalar.copy, w0_w[:], w0_raw[:], 4)
 
         a_sb = [sbuf("a%d" % t, [P, J], F32) for t in range(PACK)]
         h1 = [sbuf("h%d" % t, [P, I], F32) for t in range(PACK)]
@@ -128,17 +130,12 @@ def tile_list_ownseats_leaned_further_plain_kernel(
             if t > 0:
                 nc.scalar.activation(pw[t - 1][:].indirect(l4[:]), h1[t - 1][:], ACT.Copy)
 
-        w2_w = sbuf("w2_w", [P, R], U32)
-        w0_w = sbuf("w0_w", [P, R], U32)
         w20_s = sbuf("w20_s", [P, 2 * R], U8)
         og_s = sbuf("og_s", [P, J], U8)
         og_w = sbuf("og_w", [P, J], U32)
-        spread(w20_sr, w20_st)
-        deal(nc.gpsimd.tensor_copy, w2_w[:], w2_raw[:], 4)
-        deal(nc.gpsimd.tensor_copy, w0_w[:], w0_raw[:], 4)
-        deal(nc.gpsimd.tensor_copy, w20_s[:, 0:R], w20_sr[:, 0:R], 16)
-        deal(nc.gpsimd.tensor_copy, w20_s[:, R:], w20_sr[:, R:], 16)
         nc.vector.tensor_copy(og_w[:], xo_w[:].indirect(l2[:]))
+        deal(nc.vector.tensor_copy, w20_s[:, 0:R], w2_sr[:], 16)
+        deal(nc.vector.tensor_copy, w20_s[:, R:], w0_sr[:], 16)
         nc.vector.tensor_copy(og_s[:], xo_s[:].indirect(l2[:]))
         b_sb = [sbuf("b%d" % t, [P, J], F32) for t in range(PACK)]
         for t in range(PACK):

@@ -48,103 +48,112 @@ def tile_list_ownseats_leaned_further_plain_kernel(
         def stage_rows(dst, src, eng):
             eng.dma_start(dst, src[0].bitcast(I32).rearrange("(q r) w -> r q w", r=4))
 
-        def spread(plane, staged):
+        def spread(pairs):
             for q in range(4):
-                nc.vector.tensor_copy(plane[32 * q : 32 * q + 4, :].bitcast(I32), staged[:, q, :])
+                for plane, staged in pairs:
+                    nc.vector.tensor_copy(plane[32 * q : 32 * q + 4, :].bitcast(I32), staged[:, q, :])
 
         xt_s = sbuf("xt_s", [P, T], U8)
         xo_s = sbuf("xo_s", [P, Z], U8)
-        w_sr = sbuf("w_sr", [P, R], U8)
+        w_sr = keep.tile([P, R], U8, name="w_sr", tag="w_then_w2", align_bytes=64)
         w2_sr = sbuf("w2_sr", [P, R], U8)
         w0_sr = sbuf("w0_sr", [P, R], U8)
         wbs_s = sbuf("wbs_s", [P, 2 * N], U8)
         pw = [sbuf("pw%d" % t, [P, C], F32) for t in range(PACK)]
-        for plane in (xt_s, w_sr, xo_s, w2_sr, w0_sr, wbs_s):
+        for plane in (w0_sr, w_sr, xt_s, w2_sr, xo_s, wbs_s):
             nc.vector.memset(plane[:].bitcast(I32), 0)
         for t in range(PACK):
-            nc.vector.memset(pw[t][:], 0.0)
+            (nc.vector if t < 2 else nc.gpsimd).memset(pw[t][:], 0.0)
 
         xt_w = sbuf("xt_w", [P, T], U32)
         xo_w = sbuf("xo_w", [P, Z], U32)
         w_raw = sbuf("w_raw", [P, R], U16)
         w2_raw = sbuf("w2_raw", [P, R], U32)
-        w0_raw = sbuf("w0_raw", [P, R], U32)
+        w0_raw = keep.tile([P, R], U32, name="w0_raw", tag="w0_then_h0", align_bytes=64)
         wb_w = sbuf("wb_w", [P, N], U16)
         ws_w = sbuf("ws_w", [P, N], U16)
         w_st = sbuf("w_st", [4, 4, R // 4], I32)
         sa_t = sbuf("sa_t", [P, PACK], F32)
         sb_t = sbuf("sb_t", [P, PACK], F32)
 
-        l1 = load_list("l1", offs)
+        xt_st = sbuf("xt_st", [4, 4, T // 4], I32)
+        stage_rows(xt_st[:], xt_scales, nc.sync)
         stage_rows(w_st[:], w_scales, nc.scalar)
-        nc.sync.dma_start(w_raw[:].bitcast(I32), w_words[0].bitcast(I32))
-        nc.scalar.dma_start(sa_t[:], sa.rearrange("(p t) o -> p (t o)", t=PACK))
-        nc.scalar.dma_start(xt_w[:].bitcast(I32), fp8_rows(xt_words))
-        load_plane(xt_s[:], xt_scales, nc.sync)
+        l1 = load_list("l1", offs)
+        nc.scalar.dma_start(w_raw[:].bitcast(I32), w_words[0].bitcast(I32))
+        nc.sync.dma_start(xt_w[:].bitcast(I32), fp8_rows(xt_words))
+        l7 = load_list("l7", offs7)
         l3 = load_list("l3", offs3)
         l4 = load_list("l4", offs4)
-        l2 = load_list("l2", offs2)
-        l7 = load_list("l7", offs7)
+        load_plane(w0_sr[:], w0_scales, nc.gpsimd)
         nc.sync.dma_start(w2_raw[:].bitcast(I32), fp8_rows(w2_words))
         nc.sync.dma_start(w0_raw[:].bitcast(I32), fp8_rows(w0_words))
-        nc.sync.dma_start(xo_w[:].bitcast(I32), fp8_rows(xo_words))
+        nc.sync.dma_start(sa_t[:], sa.rearrange("(p t) o -> p (t o)", t=PACK))
+        l2 = load_list("l2", offs2)
         load_plane(w2_sr[:], w2_scales, nc.sync)
-        load_plane(w0_sr[:], w0_scales, nc.sync)
+        nc.sync.dma_start(xo_w[:].bitcast(I32), fp8_rows(xo_words))
         load_plane(xo_s[:], xo_scales, nc.sync)
         l6 = load_list("l6", offs6)
+        nc.sync.dma_start(sb_t[:], sb.rearrange("(p t) o -> p (t o)", t=PACK))
         l5 = load_list("l5", offs5)
-        nc.gpsimd.dma_start(sb_t[:], sb.rearrange("(p t) o -> p (t o)", t=PACK))
         nc.sync.dma_start(ws_w[:].bitcast(I32), ws_words[0].bitcast(I32))
         nc.sync.dma_start(wb_w[:].bitcast(I32), wb_words[0].bitcast(I32))
         load_plane(wbs_s[:, N:], ws_scales, nc.sync)
-        load_plane(wbs_s[:, 0:N], wb_scales, nc.sync)
+        load_plane(wbs_s[:, 0:N], wb_scales, nc.sync, nc.gpsimd)
 
-        def deal(copy, dst, src, line):
-            copy(dst.rearrange("p (t c i) -> p c t i", t=PACK, i=line), src.rearrange("p (c i t) -> p c t i", t=PACK, i=line))
+        def deal(copy, dst, src, line, ts=slice(0, PACK)):
+            copy(dst.rearrange("p (t c i) -> p c t i", c=P // line, i=line),
+                 src.rearrange("p (c i t) -> p c t i", t=PACK, i=line)[:, :, ts, :])
 
         xg_s = sbuf("xg_s", [P, J], U8)
         xg_w = sbuf("xg_w", [P, J], U32)
-        w_s = sbuf("w_s", [P, R], U8)
         w_w = sbuf("w_w", [P, R], U16)
         deal(nc.scalar.copy, w_w[:], w_raw[:], 8)
-        spread(w_sr, w_st)
-        deal(nc.vector.tensor_copy, w_s[:], w_sr[:], 16)
-        nc.vector.tensor_copy(xg_s[:], xt_s[:].indirect(l1[:]))
+        spread([(w_sr, w_st), (xt_s, xt_st)])
+        w_s = keep.tile([P, 2 * P], U8, name="w_s", tag="dealt_s", align_bytes=64)
+        deal(nc.vector.tensor_copy, w_s[:], w_sr[:], 16, slice(0, 2))
         nc.vector.tensor_copy(xg_w[:], xt_w[:].indirect(l1[:]))
+        nc.vector.tensor_copy(xg_s[:], xt_s[:].indirect(l1[:]))
         w2_w = sbuf("w2_w", [P, R], U32)
         w0_w = sbuf("w0_w", [P, R], U32)
         deal(nc.scalar.copy, w2_w[:], w2_raw[:], 4)
         deal(nc.scalar.copy, w0_w[:], w0_raw[:], 4)
 
-        a_sb = [sbuf("a%d" % t, [P, J], F32) for t in range(PACK)]
-        h1 = [sbuf("h%d" % t, [P, I], F32) for t in range(PACK)]
+        a_sb = [keep.tile([P, J], F32, name="a0", tag="w0_then_h0", align_bytes=64)]
+        a_sb.extend(sbuf("a%d" % t, [P, J], F32) for t in range(1, PACK))
+        h_first = keep.tile([P, PACK - 1, I], F32, name="h_first", tag="h_then_bs", align_bytes=64)
+        h_last = sbuf("h_last", [P, I], F32)
+        h1 = [h_first[:, t, :] for t in range(PACK - 1)] + [h_last[:]]
         for t in range(PACK):
             cols = slice(P * t, P * (t + 1))
+            if t == 2:
+                w_s = keep.tile([P, 2 * P], U8, name="w_s", tag="dealt_s", align_bytes=64)
+                deal(nc.vector.tensor_copy, w_s[:], w_sr[:], 16, slice(2, PACK))
             acc = psum.tile([P, J], F32, name="acc", tag="acc", bufs=6)
-            nc.tensor.matmul_mx(acc[:], lhsT=w_w[:, cols].bitcast(E2M1), lhsT_scale=w_s[:, cols],
+            nc.tensor.matmul_mx(acc[:], lhsT=w_w[:, cols].bitcast(E2M1), lhsT_scale=w_s[:, P * (t % 2) : P * (t % 2 + 1)],
                                 rhs=xg_w[:].bitcast(E5M2), rhs_scale=xg_s[:], start=True, stop=True)
-            nc.vector.tensor_copy(a_sb[t][:], acc[:])
+            (nc.scalar.copy if t == 0 else nc.vector.tensor_copy)(a_sb[t][:], acc[:])
         for t in range(PACK + 1):
             if t < PACK:
-                nc.scalar.activation(h1[t][:], a_sb[t][:].indirect(l3[:]), ACT.Copy, scale=sa_t[:, t : t + 1])
+                nc.scalar.activation(h1[t], a_sb[t][:].indirect(l3[:]), ACT.Copy, scale=sa_t[:, t : t + 1])
             if t > 0:
-                nc.scalar.activation(pw[t - 1][:].indirect(l4[:]), h1[t - 1][:], ACT.Copy)
+                nc.scalar.activation(pw[t - 1][:].indirect(l4[:]), h1[t - 1], ACT.Copy)
 
-        w20_s = sbuf("w20_s", [P, 2 * R], U8)
+        w2_s = keep.tile([P, R], U8, name="w2_s", tag="w_then_w2", align_bytes=64)
+        w0_s = keep.tile([P, R], U8, name="w0_s", tag="dealt_s", align_bytes=64)
         og_s = sbuf("og_s", [P, J], U8)
         og_w = sbuf("og_w", [P, J], U32)
+        deal(nc.vector.tensor_copy, w2_s[:], w2_sr[:], 16)
         nc.vector.tensor_copy(og_w[:], xo_w[:].indirect(l2[:]))
-        deal(nc.vector.tensor_copy, w20_s[:, 0:R], w2_sr[:], 16)
-        deal(nc.vector.tensor_copy, w20_s[:, R:], w0_sr[:], 16)
         nc.vector.tensor_copy(og_s[:], xo_s[:].indirect(l2[:]))
+        deal(nc.vector.tensor_copy, w0_s[:], w0_sr[:], 16)
         b_sb = [sbuf("b%d" % t, [P, J], F32) for t in range(PACK)]
         for t in range(PACK):
             cols = slice(P * t, P * (t + 1))
-            cols0 = slice(R + P * t, R + P * (t + 1))
             acc = psum.tile([P, J], F32, name="acc", tag="acc", bufs=6)
-            nc.tensor.matmul_mx(acc[:], lhsT=w2_w[:, cols].bitcast(E4M3), lhsT_scale=w20_s[:, cols],
+            nc.tensor.matmul_mx(acc[:], lhsT=w2_w[:, cols].bitcast(E4M3), lhsT_scale=w2_s[:, cols],
                                 rhs=xg_w[:].bitcast(E5M2), rhs_scale=xg_s[:], start=True, stop=False)
-            nc.tensor.matmul_mx(acc[:], lhsT=w0_w[:, cols].bitcast(E4M3), lhsT_scale=w20_s[:, cols0],
+            nc.tensor.matmul_mx(acc[:], lhsT=w0_w[:, cols].bitcast(E4M3), lhsT_scale=w0_s[:, cols],
                                 rhs=og_w[:].bitcast(E4M3), rhs_scale=og_s[:], start=False, stop=True)
             nc.vector.tensor_copy(b_sb[t][:], acc[:])
 
@@ -158,11 +167,11 @@ def tile_list_ownseats_leaned_further_plain_kernel(
                                 lhsT_scale=wbs_s[:, N + P * h : N + P * (h + 1)],
                                 rhs=sg_w[:].bitcast(E5M2), rhs_scale=sg_s[:], start=True, stop=False)
 
-        bs = [sbuf("bs%d" % t, [P, O], F32) for t in range(PACK)]
+        bs = keep.tile([P, PACK, O], F32, name="bs", tag="h_then_bs", align_bytes=64)
         diff = sbuf("diff", [P, PACK, O], F32)
         for t in range(PACK):
-            nc.scalar.activation(bs[t][:], b_sb[t][:].indirect(l6[:]), ACT.Copy, scale=sb_t[:, t : t + 1])
-            nc.vector.tensor_tensor(diff[:, t, :], pw[t][:].indirect(l5[:]), bs[t][:], ALU.subtract)
+            nc.scalar.activation(bs[:, t, :], b_sb[t][:].indirect(l6[:]), ACT.Copy, scale=sb_t[:, t : t + 1])
+            nc.vector.tensor_tensor(diff[:, t, :], pw[t][:].indirect(l5[:]), bs[:, t, :], ALU.subtract)
         hid = sbuf("hid", [P, O, PACK], BF16)
         woven = diff[:].rearrange("p t o -> p o t")
         half = O // 2

@@ -55,82 +55,78 @@ def tile_list_ownseats_leaned_further_plain_kernel(
 
         xt_s = sbuf("xt_s", [P, T], U8)
         xo_s = sbuf("xo_s", [P, Z], U8)
-        w_sr = keep.tile([P, R], U8, name="w_sr", tag="w_then_w2", align_bytes=64)
+        w_sr = sbuf("w_sr", [P, R], U8)
         w2_sr = sbuf("w2_sr", [P, R], U8)
         w0_sr = sbuf("w0_sr", [P, R], U8)
         wbs_s = sbuf("wbs_s", [P, 2 * N], U8)
         pw = [sbuf("pw%d" % t, [P, C], F32) for t in range(PACK)]
-        for plane in (w0_sr, w_sr, xt_s, w2_sr, xo_s, wbs_s):
+        for plane in (xt_s, w_sr, w2_sr, w0_sr, xo_s, wbs_s):
             nc.vector.memset(plane[:].bitcast(I32), 0)
         for t in range(PACK):
-            (nc.vector if t < 2 else nc.gpsimd).memset(pw[t][:], 0.0)
+            nc.vector.memset(pw[t][:], 0.0)
 
         xt_w = sbuf("xt_w", [P, T], U32)
         xo_w = sbuf("xo_w", [P, Z], U32)
         w_raw = sbuf("w_raw", [P, R], U16)
         w2_raw = sbuf("w2_raw", [P, R], U32)
-        w0_raw = keep.tile([P, R], U32, name="w0_raw", tag="w0_then_h0", align_bytes=64)
+        w0_raw = keep.tile([P, R], U32, name="w0_raw", tag="w0_then_a0", align_bytes=64)
         wb_w = sbuf("wb_w", [P, N], U16)
         ws_w = sbuf("ws_w", [P, N], U16)
         w_st = sbuf("w_st", [4, 4, R // 4], I32)
         sa_t = sbuf("sa_t", [P, PACK], F32)
         sb_t = sbuf("sb_t", [P, PACK], F32)
 
-        xt_st = sbuf("xt_st", [4, 4, T // 4], I32)
-        stage_rows(xt_st[:], xt_scales, nc.sync)
-        stage_rows(w_st[:], w_scales, nc.scalar)
         l1 = load_list("l1", offs)
-        nc.scalar.dma_start(w_raw[:].bitcast(I32), w_words[0].bitcast(I32))
-        nc.sync.dma_start(xt_w[:].bitcast(I32), fp8_rows(xt_words))
-        l7 = load_list("l7", offs7)
+        stage_rows(w_st[:], w_scales, nc.scalar)
+        nc.sync.dma_start(w_raw[:].bitcast(I32), w_words[0].bitcast(I32))
+        nc.scalar.dma_start(sa_t[:], sa.rearrange("(p t) o -> p (t o)", t=PACK))
+        nc.scalar.dma_start(xt_w[:].bitcast(I32), fp8_rows(xt_words))
+        load_plane(xt_s[:], xt_scales, nc.sync)
         l3 = load_list("l3", offs3)
-        l4 = load_list("l4", offs4)
-        load_plane(w0_sr[:], w0_scales, nc.gpsimd)
         nc.sync.dma_start(w2_raw[:].bitcast(I32), fp8_rows(w2_words))
         nc.sync.dma_start(w0_raw[:].bitcast(I32), fp8_rows(w0_words))
-        nc.sync.dma_start(sa_t[:], sa.rearrange("(p t) o -> p (t o)", t=PACK))
+        l4 = load_list("l4", offs4)
+        l7 = load_list("l7", offs7)
+        nc.gpsimd.dma_start(sb_t[:], sb.rearrange("(p t) o -> p (t o)", t=PACK))
+        nc.sync.dma_start(xo_w[:].bitcast(I32), fp8_rows(xo_words))
         l2 = load_list("l2", offs2)
         load_plane(w2_sr[:], w2_scales, nc.sync)
-        nc.sync.dma_start(xo_w[:].bitcast(I32), fp8_rows(xo_words))
+        load_plane(w0_sr[:], w0_scales, nc.sync)
         load_plane(xo_s[:], xo_scales, nc.sync)
         l6 = load_list("l6", offs6)
-        nc.sync.dma_start(sb_t[:], sb.rearrange("(p t) o -> p (t o)", t=PACK))
         l5 = load_list("l5", offs5)
         nc.sync.dma_start(ws_w[:].bitcast(I32), ws_words[0].bitcast(I32))
         nc.sync.dma_start(wb_w[:].bitcast(I32), wb_words[0].bitcast(I32))
         load_plane(wbs_s[:, N:], ws_scales, nc.sync)
-        load_plane(wbs_s[:, 0:N], wb_scales, nc.sync, nc.gpsimd)
+        load_plane(wbs_s[:, 0:N], wb_scales, nc.sync)
 
-        def deal(copy, dst, src, line, ts=slice(0, PACK)):
+        def deal(copy, dst, src, line):
             copy(dst.rearrange("p (t c i) -> p c t i", c=P // line, i=line),
-                 src.rearrange("p (c i t) -> p c t i", t=PACK, i=line)[:, :, ts, :])
+                 src.rearrange("p (c i t) -> p c t i", t=PACK, i=line))
 
         xg_s = sbuf("xg_s", [P, J], U8)
         xg_w = sbuf("xg_w", [P, J], U32)
-        w_w = sbuf("w_w", [P, R], U16)
+        w_w = keep.tile([P, R], U16, name="w_w", tag="w_then_og", align_bytes=64)
         deal(nc.scalar.copy, w_w[:], w_raw[:], 8)
-        spread([(w_sr, w_st), (xt_s, xt_st)])
-        w_s = keep.tile([P, 2 * P], U8, name="w_s", tag="dealt_s", align_bytes=64)
-        deal(nc.vector.tensor_copy, w_s[:], w_sr[:], 16, slice(0, 2))
+        spread([(w_sr, w_st)])
+        w_s = keep.tile([P, R], U8, name="w_s", tag="dealt_s", align_bytes=64)
+        deal(nc.vector.tensor_copy, w_s[:], w_sr[:], 16)
         nc.vector.tensor_copy(xg_w[:], xt_w[:].indirect(l1[:]))
         nc.vector.tensor_copy(xg_s[:], xt_s[:].indirect(l1[:]))
+
         w2_w = sbuf("w2_w", [P, R], U32)
-        w0_w = sbuf("w0_w", [P, R], U32)
+        w0_w = keep.tile([P, R], U32, name="w0_w", tag="w0_then_diff", align_bytes=64)
         deal(nc.scalar.copy, w2_w[:], w2_raw[:], 4)
         deal(nc.scalar.copy, w0_w[:], w0_raw[:], 4)
-
-        a_sb = [keep.tile([P, J], F32, name="a0", tag="w0_then_h0", align_bytes=64)]
-        a_sb.extend(sbuf("a%d" % t, [P, J], F32) for t in range(1, PACK))
+        a_tags = ["w0_then_a0", "a1_then_og", "a2", "a3"]
+        a_sb = [keep.tile([P, J], F32, name="a%d" % t, tag=a_tags[t], align_bytes=64) for t in range(PACK)]
         h_first = keep.tile([P, PACK - 1, I], F32, name="h_first", tag="h_then_bs", align_bytes=64)
         h_last = sbuf("h_last", [P, I], F32)
         h1 = [h_first[:, t, :] for t in range(PACK - 1)] + [h_last[:]]
         for t in range(PACK):
             cols = slice(P * t, P * (t + 1))
-            if t == 2:
-                w_s = keep.tile([P, 2 * P], U8, name="w_s", tag="dealt_s", align_bytes=64)
-                deal(nc.vector.tensor_copy, w_s[:], w_sr[:], 16, slice(2, PACK))
             acc = psum.tile([P, J], F32, name="acc", tag="acc", bufs=6)
-            nc.tensor.matmul_mx(acc[:], lhsT=w_w[:, cols].bitcast(E2M1), lhsT_scale=w_s[:, P * (t % 2) : P * (t % 2 + 1)],
+            nc.tensor.matmul_mx(acc[:], lhsT=w_w[:, cols].bitcast(E2M1), lhsT_scale=w_s[:, cols],
                                 rhs=xg_w[:].bitcast(E5M2), rhs_scale=xg_s[:], start=True, stop=True)
             (nc.scalar.copy if t == 0 else nc.vector.tensor_copy)(a_sb[t][:], acc[:])
         for t in range(PACK + 1):
@@ -139,14 +135,15 @@ def tile_list_ownseats_leaned_further_plain_kernel(
             if t > 0:
                 nc.scalar.activation(pw[t - 1][:].indirect(l4[:]), h1[t - 1], ACT.Copy)
 
-        w2_s = keep.tile([P, R], U8, name="w2_s", tag="w_then_w2", align_bytes=64)
-        w0_s = keep.tile([P, R], U8, name="w0_s", tag="dealt_s", align_bytes=64)
-        og_s = sbuf("og_s", [P, J], U8)
-        og_w = sbuf("og_w", [P, J], U32)
-        deal(nc.vector.tensor_copy, w2_s[:], w2_sr[:], 16)
+        w20_s = keep.tile([P, 2 * R], U8, name="w20_s", tag="dealt_s", align_bytes=64)
+        w2_s = w20_s[:, 0:R]
+        w0_s = w20_s[:, R:]
+        og_s = keep.tile([P, J], U8, name="og_s", tag="a1_then_og", align_bytes=64)
+        og_w = keep.tile([P, J], U32, name="og_w", tag="w_then_og", align_bytes=64)
+        deal(nc.vector.tensor_copy, w2_s, w2_sr[:], 16)
         nc.vector.tensor_copy(og_w[:], xo_w[:].indirect(l2[:]))
+        deal(nc.vector.tensor_copy, w0_s, w0_sr[:], 16)
         nc.vector.tensor_copy(og_s[:], xo_s[:].indirect(l2[:]))
-        deal(nc.vector.tensor_copy, w0_s[:], w0_sr[:], 16)
         b_sb = [sbuf("b%d" % t, [P, J], F32) for t in range(PACK)]
         for t in range(PACK):
             cols = slice(P * t, P * (t + 1))
@@ -168,7 +165,7 @@ def tile_list_ownseats_leaned_further_plain_kernel(
                                 rhs=sg_w[:].bitcast(E5M2), rhs_scale=sg_s[:], start=True, stop=False)
 
         bs = keep.tile([P, PACK, O], F32, name="bs", tag="h_then_bs", align_bytes=64)
-        diff = sbuf("diff", [P, PACK, O], F32)
+        diff = keep.tile([P, PACK, O], F32, name="diff", tag="w0_then_diff", align_bytes=64)
         for t in range(PACK):
             nc.scalar.activation(bs[:, t, :], b_sb[t][:].indirect(l6[:]), ACT.Copy, scale=sb_t[:, t : t + 1])
             nc.vector.tensor_tensor(diff[:, t, :], pw[t][:].indirect(l5[:]), bs[:, t, :], ALU.subtract)

from contextlib import ExitStack

import concourse.mybir as mybir

F32 = mybir.dt.float32
BF16 = mybir.dt.bfloat16
I32 = mybir.dt.int32
U32 = mybir.dt.uint32
U16 = mybir.dt.uint16
U8 = mybir.dt.uint8
E4M3 = mybir.dt.float8_e4m3fn_x4
E5M2 = mybir.dt.float8_e5m2_x4
E2M1 = mybir.dt.float4_e2m1fn_x4
ALU = mybir.AluOpType
ACT = mybir.ActivationFunctionType

K, T, J, R, F, Z, C, I, O, N = 512, 1024, 256, 512, 512, 1024, 512, 128, 128, 256
P = 128
PACK = 4
FLOPS = 2 * (3 * K * R * J + R * N * O + K * N * O)


def tile_list_ownseats_leaned_further_plain_kernel(
    tc, xt_words, xt_scales, xo_words, xo_scales, w_words, w_scales, w2_words, w2_scales, w0_words, w0_scales,
    sa, sb, wb_words, wb_scales, ws_words, ws_scales, offs, offs2, offs3, offs4, offs5, offs6, offs7, out,
):
    nc = tc.nc
    with ExitStack() as ctx:
        keep = ctx.enter_context(tc.tile_pool(name="keep", bufs=1))
        psum = ctx.enter_context(tc.psum_pool(name="psum", bufs=1))

        def sbuf(name, shape, dtype):
            return keep.tile(shape, dtype, name=name, align_bytes=64)

        def load_list(name, src):
            t = keep.tile(list(src.shape), U16, name=name)
            nc.sync.dma_start(t[:], src)
            return t

        def fp8_rows(src):
            return src[0].rearrange("p c r -> p (c r)").bitcast(I32)

        def load_plane(plane, src, *engs):
            rows = src[0].bitcast(I32)
            for q in range(4):
                engs[q % len(engs)].dma_start(plane[32 * q : 32 * q + 4].bitcast(I32), rows[4 * q : 4 * q + 4, :])

        def stage_rows(dst, src, eng):
            eng.dma_start(dst, src[0].bitcast(I32).rearrange("(q r) w -> r q w", r=4))

        def spread(pairs):
            for q in range(4):
                for plane, staged in pairs:
                    nc.vector.tensor_copy(plane[32 * q : 32 * q + 4, :].bitcast(I32), staged[:, q, :])

        xt_s = sbuf("xt_s", [P, T], U8)
        xo_s = sbuf("xo_s", [P, Z], U8)
        w_sr = sbuf("w_sr", [P, R], U8)
        w2_sr = sbuf("w2_sr", [P, R], U8)
        w0_sr = sbuf("w0_sr", [P, R], U8)
        wbs_s = sbuf("wbs_s", [P, 2 * N], U8)
        pw = [sbuf("pw%d" % t, [P, C], F32) for t in range(PACK)]
        for plane in (xt_s, w_sr, w2_sr, w0_sr, xo_s, wbs_s):
            nc.vector.memset(plane[:].bitcast(I32), 0)
        for t in range(PACK):
            nc.vector.memset(pw[t][:], 0.0)

        xt_w = sbuf("xt_w", [P, T], U32)
        xo_w = sbuf("xo_w", [P, Z], U32)
        w_raw = sbuf("w_raw", [P, R], U16)
        w2_raw = sbuf("w2_raw", [P, R], U32)
        w0_raw = keep.tile([P, R], U32, name="w0_raw", tag="w0_then_a0", align_bytes=64)
        wb_w = sbuf("wb_w", [P, N], U16)
        ws_w = sbuf("ws_w", [P, N], U16)
        w_st = sbuf("w_st", [4, 4, R // 4], I32)
        sa_t = sbuf("sa_t", [P, PACK], F32)
        sb_t = sbuf("sb_t", [P, PACK], F32)

        l1 = load_list("l1", offs)
        stage_rows(w_st[:], w_scales, nc.scalar)
        nc.sync.dma_start(w_raw[:].bitcast(I32), w_words[0].bitcast(I32))
        nc.scalar.dma_start(sa_t[:], sa.rearrange("(p t) o -> p (t o)", t=PACK))
        nc.scalar.dma_start(xt_w[:].bitcast(I32), fp8_rows(xt_words))
        load_plane(xt_s[:], xt_scales, nc.sync)
        l3 = load_list("l3", offs3)
        nc.sync.dma_start(w2_raw[:].bitcast(I32), fp8_rows(w2_words))
        nc.sync.dma_start(w0_raw[:].bitcast(I32), fp8_rows(w0_words))
        l4 = load_list("l4", offs4)
        l7 = load_list("l7", offs7)
        nc.gpsimd.dma_start(sb_t[:], sb.rearrange("(p t) o -> p (t o)", t=PACK))
        nc.sync.dma_start(xo_w[:].bitcast(I32), fp8_rows(xo_words))
        l2 = load_list("l2", offs2)
        load_plane(w2_sr[:], w2_scales, nc.sync)
        load_plane(w0_sr[:], w0_scales, nc.sync)
        load_plane(xo_s[:], xo_scales, nc.sync)
        l6 = load_list("l6", offs6)
        l5 = load_list("l5", offs5)
        nc.sync.dma_start(ws_w[:].bitcast(I32), ws_words[0].bitcast(I32))
        nc.sync.dma_start(wb_w[:].bitcast(I32), wb_words[0].bitcast(I32))
        load_plane(wbs_s[:, N:], ws_scales, nc.sync)
        load_plane(wbs_s[:, 0:N], wb_scales, nc.sync)

        def deal(copy, dst, src, line):
            copy(dst.rearrange("p (t c i) -> p c t i", c=P // line, i=line),
                 src.rearrange("p (c i t) -> p c t i", t=PACK, i=line))

        xg_s = sbuf("xg_s", [P, J], U8)
        xg_w = sbuf("xg_w", [P, J], U32)
        w_w = keep.tile([P, R], U16, name="w_w", tag="w_then_og", align_bytes=64)
        deal(nc.scalar.copy, w_w[:], w_raw[:], 8)
        spread([(w_sr, w_st)])
        w_s = keep.tile([P, R], U8, name="w_s", tag="dealt_s", align_bytes=64)
        deal(nc.vector.tensor_copy, w_s[:], w_sr[:], 16)
        nc.vector.tensor_copy(xg_w[:], xt_w[:].indirect(l1[:]))
        nc.vector.tensor_copy(xg_s[:], xt_s[:].indirect(l1[:]))

        w2_w = sbuf("w2_w", [P, R], U32)
        w0_w = keep.tile([P, R], U32, name="w0_w", tag="w0_then_diff", align_bytes=64)
        deal(nc.scalar.copy, w2_w[:], w2_raw[:], 4)
        deal(nc.scalar.copy, w0_w[:], w0_raw[:], 4)
        a_tags = ["w0_then_a0", "a1_then_og", "a2", "a3"]
        a_sb = [keep.tile([P, J], F32, name="a%d" % t, tag=a_tags[t], align_bytes=64) for t in range(PACK)]
        h_first = keep.tile([P, PACK - 1, I], F32, name="h_first", tag="h_then_bs", align_bytes=64)
        h_last = sbuf("h_last", [P, I], F32)
        h1 = [h_first[:, t, :] for t in range(PACK - 1)] + [h_last[:]]
        for t in range(PACK):
            cols = slice(P * t, P * (t + 1))
            acc = psum.tile([P, J], F32, name="acc", tag="acc", bufs=6)
            nc.tensor.matmul_mx(acc[:], lhsT=w_w[:, cols].bitcast(E2M1), lhsT_scale=w_s[:, cols],
                                rhs=xg_w[:].bitcast(E5M2), rhs_scale=xg_s[:], start=True, stop=True)
            (nc.scalar.copy if t == 0 else nc.vector.tensor_copy)(a_sb[t][:], acc[:])
        for t in range(PACK + 1):
            if t < PACK:
                nc.scalar.activation(h1[t], a_sb[t][:].indirect(l3[:]), ACT.Copy, scale=sa_t[:, t : t + 1])
            if t > 0:
                nc.scalar.activation(pw[t - 1][:].indirect(l4[:]), h1[t - 1], ACT.Copy)

        w20_s = keep.tile([P, 2 * R], U8, name="w20_s", tag="dealt_s", align_bytes=64)
        w2_s = w20_s[:, 0:R]
        w0_s = w20_s[:, R:]
        og_s = keep.tile([P, J], U8, name="og_s", tag="a1_then_og", align_bytes=64)
        og_w = keep.tile([P, J], U32, name="og_w", tag="w_then_og", align_bytes=64)
        deal(nc.vector.tensor_copy, w2_s, w2_sr[:], 16)
        nc.vector.tensor_copy(og_w[:], xo_w[:].indirect(l2[:]))
        deal(nc.vector.tensor_copy, w0_s, w0_sr[:], 16)
        nc.vector.tensor_copy(og_s[:], xo_s[:].indirect(l2[:]))
        b_sb = [sbuf("b%d" % t, [P, J], F32) for t in range(PACK)]
        for t in range(PACK):
            cols = slice(P * t, P * (t + 1))
            acc = psum.tile([P, J], F32, name="acc", tag="acc", bufs=6)
            nc.tensor.matmul_mx(acc[:], lhsT=w2_w[:, cols].bitcast(E4M3), lhsT_scale=w2_s[:, cols],
                                rhs=xg_w[:].bitcast(E5M2), rhs_scale=xg_s[:], start=True, stop=False)
            nc.tensor.matmul_mx(acc[:], lhsT=w0_w[:, cols].bitcast(E4M3), lhsT_scale=w0_s[:, cols],
                                rhs=og_w[:].bitcast(E4M3), rhs_scale=og_s[:], start=False, stop=True)
            nc.vector.tensor_copy(b_sb[t][:], acc[:])

        sg_s = sbuf("sg_s", [P, O], U8)
        sg_w = sbuf("sg_w", [P, O], U32)
        nc.vector.tensor_copy(sg_w[:], xt_w[:].indirect(l7[:]))
        nc.vector.tensor_copy(sg_s[:], xt_s[:].indirect(l7[:]))
        y = [psum.tile([P, O], F32, name="y%d" % h) for h in range(N // P)]
        for h in range(N // P):
            nc.tensor.matmul_mx(y[h][:], lhsT=ws_w[:, P * h : P * (h + 1)].bitcast(E2M1),
                                lhsT_scale=wbs_s[:, N + P * h : N + P * (h + 1)],
                                rhs=sg_w[:].bitcast(E5M2), rhs_scale=sg_s[:], start=True, stop=False)

        bs = keep.tile([P, PACK, O], F32, name="bs", tag="h_then_bs", align_bytes=64)
        diff = keep.tile([P, PACK, O], F32, name="diff", tag="w0_then_diff", align_bytes=64)
        for t in range(PACK):
            nc.scalar.activation(bs[:, t, :], b_sb[t][:].indirect(l6[:]), ACT.Copy, scale=sb_t[:, t : t + 1])
            nc.vector.tensor_tensor(diff[:, t, :], pw[t][:].indirect(l5[:]), bs[:, t, :], ALU.subtract)
        hid = sbuf("hid", [P, O, PACK], BF16)
        woven = diff[:].rearrange("p t o -> p o t")
        half = O // 2
        nc.scalar.activation(hid[:, 0:half, :], woven[:, 0:half, :], ACT.Abs)
        nc.vector.scalar_tensor_tensor(hid[:, half:, :], woven[:, half:, :], -1.0, woven[:, half:, :], ALU.mult, ALU.max)
        hq_w = sbuf("hq_w", [P, O], U32)
        hq_s = sbuf("hq_s", [P, O], U8)
        nc.vector.quantize_mx(hq_w[:].bitcast(E4M3), hq_s[:], hid[:].rearrange("p o t -> p (o t)"))
        y_sb = [sbuf("ysb%d" % h, [P, O], F32) for h in range(N // P)]
        for h in range(N // P):
            nc.tensor.matmul_mx(y[h][:], lhsT=wb_w[:, P * h : P * (h + 1)].bitcast(E2M1),
                                lhsT_scale=wbs_s[:, P * h : P * (h + 1)],
                                rhs=hq_w[:].bitcast(E4M3), rhs_scale=hq_s[:], start=False, stop=True)
        nc.vector.tensor_copy(y_sb[0][:], y[0][:])
        nc.sync.dma_start(out[0:P, :], y_sb[0][:])
        nc.scalar.copy(y_sb[1][:], y[1][:])
        nc.scalar.dma_start(out[P:, :], y_sb[1][:])
